import numpy as np, ml_dtypes
CORES = [36,164,52,180,100,228,116,244]
N = 8
import mx_ref
BF = ml_dtypes.bfloat16
def gentries(a):
    return np.ascontiguousarray(a.reshape(8, 16, -1).transpose(0, 2, 1)).reshape(8, -1)
def gtable(e):
    e = np.asarray(e); return np.ascontiguousarray(e.reshape(8, -1, 16).transpose(0, 2, 1)).reshape(128, -1).astype(np.int32)
def gcols(t, e):
    v = np.concatenate([t.reshape(8, 16, -1, 4), np.zeros((8, 16, 1, 4), BF)], axis=2)
    return np.ascontiguousarray(np.stack([v[g][:, e[g]] for g in range(8)])).reshape(128, -1)
def tile(rs):
    return np.stack(rs, axis=2).reshape(128, -1).astype(BF)
def pick(q, e):
    c = np.concatenate([q[0].reshape(128, -1, 4), np.zeros((128, 1, 4), np.uint8)], axis=1); s = np.concatenate([q[1], np.ones((16, 1), np.uint8)], axis=1)
    return (np.ascontiguousarray(c[:, e].reshape(128, -1)), np.ascontiguousarray(s[:, e]))
def join(*qs):
    return (np.concatenate([q[0] for q in qs], axis=1), np.concatenate([q[1] for q in qs], axis=1))
def put(q, e, v):
    c, s = q[0].reshape(128, -1, 4).copy(), q[1].copy(); c[:, e] = v[0].reshape(128, -1, 4); s[:, e] = v[1]
    return (c.reshape(128, -1), s)
def pk(c, s):
    return (np.ascontiguousarray(c), mx_ref.live(s))
def emit(q):
    return q[0], q[1]
def packed(v, rng):
    q = [mx_ref.quantize(np.ascontiguousarray(v[r])) for r in range(N)]
    return np.stack([a for a, b in q]), np.stack([mx_ref.plane(b, rng) for a, b in q])
def values_of_codes():
    e, c = np.zeros((128, 128, 4), np.float32), np.zeros((128, 2, 4), np.uint8)
    e[np.arange(128), np.arange(128), 0] = 1
    c[:127, :, 0] = np.arange(256).reshape(2, 128).T[:127]
    return mx_ref.matmul(mx_ref.quantize(e.reshape(128, 512).astype(BF)), (c.reshape(128, 8), np.full((16, 2), 127, np.uint8))).T.reshape(-1).astype(np.float64)
CODE_VALUE, SCALE_VALUE = values_of_codes(), 2.0 ** (np.arange(256) - 127.0)
def decode(q):
    return (CODE_VALUE[q[0]].reshape(16, 8, -1, 4) * SCALE_VALUE[q[1]][:, None, :, None] + 0.0).reshape(128, -1).astype(np.float32)
def f(rng, *shape):
    return mx_ref.flush((rng.standard_normal(shape, dtype=np.float32) * np.exp2(rng.integers(-2, 3, shape[:-1] + (1,)))).astype(BF))
def wide(rng, *shape, cols=0):
    v = rng.standard_normal(shape, dtype=np.float32) * np.exp2(rng.integers(-12, 13, shape)).astype(np.float32)
    if cols: v *= np.repeat(np.exp2(rng.integers(-cols, cols + 1, shape[:-2] + (1, shape[-1] // 4))) * (rng.random(shape[:-2] + (1, shape[-1] // 4)) > 0.0625), 4, axis=-1).astype(np.float32)
    return mx_ref.flush(v.astype(BF))
C = 320
MASK = [4, 1, 2]
def numbers_of(rng):
    return {"x": np.array(f(rng, N, 128, 4 * C)), "u": np.array(f(rng, N, 128, 512)), "v": np.array(f(rng, N, 128, 512))}
def following(o):
    e = np.zeros_like(o)
    np.put_along_axis(e, o, np.roll(o, -1, axis=-1), axis=-1)
    return e
def rings(rng):
    return following(rng.permuted(np.tile(np.arange(C), (N, 8, 1)), axis=2))
def runs(rng, when, same=False):
    o, go = np.zeros((N, 8, C), np.int64), np.zeros((N, 8, C), bool)
    for r in range(N):
        k = rng.permutation(C)
        for g in range(8):
            p = r ^ MASK[when[g]]
            if p < r: continue
            if not same: k = rng.permutation(C)
            for i, m in ((r, [1, 0, 3, 2]), (p, [2, 0, 3, 1])):
                q = rng.permuted(k.reshape(4, -1), axis=1)[m]
                o[i, g] = np.concatenate([q[:2].T.reshape(-1), q[2:].T.reshape(-1)])
                go[i, g, q[:2].reshape(-1)] = True
    return following(o), go
def stored(e):
    return {"nx": np.stack([gtable(e[r]) for r in range(N)])}
def layers(rng, still=[]):
    w = np.array(f(rng, N, 128, 2048)).reshape(N, 8, 16, 4, 8, 16, 4)
    for i in still:
        w[:, :, i] = 0
        w[:, :, :, :, :, i] = 0
    return w
def weights(rng, w):
    c, s = packed(np.ascontiguousarray(w).reshape(N, 128, 2048), rng)
    return {"wc": c, "ws": s}
def setup_inputs(rng):
    return {**numbers_of(rng), **stored(rings(rng)), **weights(rng, layers(rng))}
def setup_inputs_ties(rng):
    d = numbers_of(rng)
    o = rng.permutation(N)
    k = rng.integers(-1, 2, (N, 8, C)).astype(np.float32)
    k[o[1]] = 1
    x = d["x"].reshape(N, 8, 16, C, 4)
    x[:, :, 0] = 0
    x[:, :, 0, :, 0] = k.astype(BF)
    c = np.ones(N, np.float32)
    c[o[0]] = 0
    c[o[2]] = -1
    u = d["u"].reshape(N, 128, 128, 4)
    u[:, :, ::16] = 0
    for h in range(0, 128, 16): u[:, h, h, 0] = c.astype(BF)
    e, i = rings(rng), np.arange(C)
    for r in range(N):
        p, h = r ^ MASK[0], rng.permutation(8)
        if p < r: continue
        e[p, h[0]] = e[r, h[0]]
        e[p, h[1]] = np.argsort(e[r, h[1]])
        e[r, h[2]], e[p, h[2]] = (i + 1) % C, (i - 1) % C
        e[r, h[3]] = e[p, h[3]] = (i + 1) % C
    w = layers(rng)
    w[:, :, :, :, :, :8] = 0
    return {"x": x.reshape(N, 128, 4 * C), "u": u.reshape(N, 128, 512), "v": d["v"], **stored(e), **weights(rng, w)}
def setup_inputs_near(rng):
    d = numbers_of(rng)
    o = rng.permutation(N) % 4
    k = np.where(o % 2 == 0, 1.0, 2.0 ** -30)
    x = np.zeros((N, 8, 16, C, 4))
    s = rng.integers(-1, 2, (N, 8, C)) * k[:, None, None]
    x[:, :, 0, :, 0] = 1.125 * s
    x[:, :, 1, :, 0] = -1.25 * s
    x[:, :, 8, :, 0] = rng.integers(-1, 2, (N, 8, C)) * 2.0 ** -27
    x[:, :, 8, :, 1] = 2.0 ** -27
    x[:, :, 9:] = (1.0 + rng.integers(0, 128, (N, 8, 7, C, 4)) * 2.0 ** -7) * 2.0 ** -27 * rng.choice([-1.0, 1.0], (N, 8, 7, C, 4))
    w = layers(rng, list(range(9)))
    for r in range(N):
        if o[r] % 2 == 1: x[r, :, 7, :, 0] = 2.0 ** -26
        if o[r] == 3:
            x[r, :, :2] = 0
            x[r, :, 7, :, 0] = 2.0 ** -27
            for g in range(8):
                w[r, g, 8, 0, g, 0, 0] = 2.0 ** -10
                w[r, g, 8, 0, g, 0, 1] = 2.0 ** -8
                w[r, g, 8, 0, g, 1, 0] = -2.0 ** -10
                w[r, g, 8, 0, g, 1, 1] = -1.125 * 2.0 ** -8
        else:
            at = [0, C - 1, int(rng.integers(C)), int(rng.integers(C))]
            for g, j in zip(rng.permutation(8)[:4], at): x[r, g, 0, j, 0] = 2.0 ** 30 * rng.choice([-1.0, 1.0])
    u = d["u"].reshape(N, 128, 128, 4)
    u[:, :, ::16] = 0
    for h in range(0, 128, 16):
        u[:, h, h, 0] = (1.125 * k).astype(np.float32).astype(BF)
        u[:, h + 1, h, 0] = k.astype(np.float32).astype(BF)
    return {"x": x.astype(np.float32).reshape(N, 128, 4 * C).astype(BF), "u": u.reshape(N, 128, 512), "v": d["v"], **stored(rings(rng)), **weights(rng, w)}
def setup_inputs_runs(rng):
    d = numbers_of(rng)
    o = rng.permutation(8)
    when = np.zeros(8, np.int64)
    when[o[4:6]] = 1
    when[o[6:]] = 2
    e, go = runs(rng, when)
    low = -rng.integers(0, 2, (N, 8, C))
    t = np.where(go, 1, low)
    for r in range(N):
        h = rng.permutation(o[:4])
        t[r, h[0]] = 1
        t[r, h[1]] = low[r, h[1]]
    for g in o[4:]:
        for i in range(when[g]): t[:, g] = np.take_along_axis(t[:, g], e[:, g], axis=1)
    x = (1.0 + (2 * rng.integers(0, 64, (N, 16, 8, C, 4)) + 1) * 2.0 ** -7) * np.exp2(-rng.integers(0, 7, (N, 16, 8, C, 4)).astype(np.float64)) * rng.choice([-1.0, 1.0], (N, 16, 8, C, 4))
    c = rng.choice([-1.0, 1.0], (N, 16, 1))
    k = np.exp2(when - 8.0)[:, None]
    x[:, :, 0, :, 0] = np.where(rng.random((N, 16, C)) < 0.5, 1.96875, 1.875) * 2.0 ** 8 * c
    x[:, :, 3, :, 0] = 1.875 * 2.0 ** 7
    x[:, ::2, 1, :, 0] = (8 + t) * k
    x[:, ::2, 2, :, 0] = 8 * k
    u = d["u"].reshape(N, 128, 128, 4)
    u[:, :, ::16] = 0
    for h in range(0, 128, 16):
        u[:, h + 1, h, 0] = 1
        u[:, h + 2, h, 0] = -1
    w = layers(rng, [0, 3, 8, 11])
    for g in range(8):
        for i in (0, 1):
            w[:, g, 8 * i + 3, 0, g, 8 * i, 0] = (64 * c[:, 2 * g + i, 0]).astype(np.float32).astype(BF)
            w[:, g, 8 * i + 3, 0, g, 8 * i + 3, 0] = 32
    for g in o[4:]:
        x[:, 2 * g, 4, :, 0] = -1.0
        x[:, 2 * g, 5, :, 0] = 1.0 - when[g]
        u[:, 16 * g + 4, 16 * g, 0] = 1
        for i in (1, 2, 4, 5): w[:, :, :, :, g, i] = 0
        w[:, g, 4, 0, g, 4, 0] = -32
        w[:, g, 5, 0, g, 4, 0] = 64
        w[:, g, 5, 0, g, 5, 0] = -32
    return {"x": x.astype(np.float32).reshape(N, 128, 4 * C).astype(BF), "u": u.reshape(N, 128, 512), "v": d["v"], **stored(e), **weights(rng, w)}
def setup_inputs_ends(rng):
    d = numbers_of(rng)
    e, go = runs(rng, np.zeros(8, np.int64), True)
    o = rng.permutation(N) % 4
    s = go[:, 0] * 2.0 - 1.0
    small = (1.0 + 0.125 * rng.integers(0, 8, (N, 8, 16, C, 4))) * 2.0 ** -20
    x = (0.9 + 0.1 * rng.random((N, 8, 16, C, 4))) * 2.0 ** 30
    u = d["u"].astype(np.float32).reshape(N, 128, 128, 4)
    v = np.zeros((N, 128, 512), np.float32)
    w = np.zeros((N, 128, 4, 128, 4), np.float32)
    i = np.arange(128)
    for r in range(N):
        if o[r] == 0: x[r] *= s[r][:, None]
        if o[r] == 1: x[r] *= -1
        if o[r] == 2: x[r] *= rng.choice([-1.0, 1.0], (8, 1, C, 1))
        if o[r] == 3: x[r] = small[r] * s[r][:, None]
        x[r, 7, 8:] = small[r, 7, 8:] * rng.choice([-1.0, 1.0], (8, C, 4))
        c = np.array([0.0, 1, 1, 1, -1, -1, -1, -1])[rng.permutation(8)][None, :, None]
        if o[r] < 3: u[r, :, ::16] = c * (0.9 + 0.1 * rng.random((128, 8, 4))) * 2.0 ** 30
        else: u[r, :, ::16] = c * (1.0 + 0.125 * rng.integers(0, 8, (128, 8, 4))) * 2.0 ** -30
        if o[r] < 2: v[r] = (0.9 + 0.1 * rng.random((128, 512))) * 2.0 ** 30
        else: v[r] = (1.0 + 0.125 * rng.integers(0, 8, (128, 512))) * 2.0 ** -30
        v[r] *= rng.choice([-1.0, 1.0], (128, 512))
        k = np.full(128, 32.0)
        if o[r] == 3: k = np.where(i < 120, 2.0 ** -8, 2.0 ** 8)
        for b in range(4): w[r, i, b, i, b] = k
    return {"x": x.astype(np.float32).reshape(N, 128, 4 * C).astype(BF), "u": u.reshape(N, 128, 512).astype(BF), "v": v.astype(BF), **stored(e), **weights(rng, w.astype(BF))}
def setup_inputs_spread(rng):
    d = setup_inputs(rng)
    d["x"] = wide(rng, N, 128, 4 * C, cols=6)
    return d
def check_inputs(d):
    b = []
    for k in ("x", "u", "v"):
        a = np.abs(d[k].astype(np.float32))
        if not (np.isfinite(a).all() and ((a == 0) | (a >= 2.0 ** -30) & (a <= 2.0 ** 30)).all()): b.append("a value of " + k)
    if not ((d["nx"] >= 0) & (d["nx"] < C)).all(): b.append("an entry of nx")
    else:
        e = np.concatenate([gentries(d["nx"][r]) for r in range(N)])
        at, back = np.zeros(8 * N, np.int64), np.zeros(8 * N, np.int64)
        for i in range(1, C + 1):
            at = e[np.arange(8 * N), at]
            back = np.where((at == 0) & (back == 0), i, back)
        if not (back == C).all(): b.append("a ring of nx")
    none, least, most = [emit(mx_ref.quantize(np.full((128, 16), k, np.float32).astype(BF)))[1][0, 0] for k in (0.0, 2.0 ** -8, 2.0 ** 8)]
    for r in range(N):
        if ((d["wc"][r] == 0x7F) | (d["wc"][r] == 0xFF)).any(): b.append("wc: a code that is no number")
        s = mx_ref.live(d["ws"][r])
        if ((s != none) & ((s < least) | (s > most))).any(): b.append("ws: a scale out of range")
    return b
def at(a, e):
    return np.take_along_axis(a, e, axis=1)
def mean(a, b):
    return ((a.astype(np.float32) + b.astype(np.float32)) * np.float32(0.5)).astype(BF)
def reference(x, u, v, nx, wc, ws):
    qu = [mx_ref.quantize(u[r]) for r in range(N)]
    lay = [pk(wc[r], ws[r]) for r in range(N)]
    ring = [gentries(nx[r]).astype(np.int64) for r in range(N)]
    now = [x[r] for r in range(N)]
    for m in MASK:
        t, new, back, z = [], [], [], []
        for r in range(N):
            q = mx_ref.quantize(now[r])
            t.append(decode(q).astype(BF))
            up = mx_ref.matmul(qu[r], q)[::16] > 0
            guest = ring[r ^ m]
            host = np.argsort(guest, axis=1)
            leave = up & ~at(up, host)
            a = ring[r]
            for i in range(8):
                a = np.where(at(leave, a), at(a, a), a)
            new.append(np.where(leave, at(a, host), np.where(at(leave, guest), guest, a)))
            back.append(np.argsort(new[r], axis=1))
            z.append(mx_ref.quantize(mean(gcols(t[r], new[r]), gcols(t[r], back[r]))))
        for r in range(N):
            h = tile([mx_ref.matmul(pick(lay[r], np.arange(128 * b, 128 * b + 128)), z[r ^ m]) * np.float32(0.03125) for b in range(4)])
            now[r] = mean(gcols(t[r], back[r]), gcols(h, new[r]))
        ring = new
    y, nr = np.zeros((N, 128, C), np.float32), np.zeros((N, 8, C), np.float32)
    oc, osc = np.zeros((N, 128, 4 * C), np.uint8), np.zeros((N, 16, C), np.uint8)
    for r in range(N):
        q = mx_ref.quantize(now[r])
        y[r] = mx_ref.matmul(mx_ref.quantize(v[r]), q)
        nr[r] = ring[r]
        oc[r], osc[r] = emit(q)
    return {"y": y, "nr": nr, "oc": oc, "osc": osc}

@@ -1,0 +1,396 @@
+from concourse.mybir import dt, AluOpType, AxisListType, ActivationFunctionType
+
+N, C, MASK = 8, 320, [4, 1, 2]
+BF, F4, F2, I4, U2, CO, PL = "bfloat16", "float32", "float16", "int32", "uint16", "float8_e4m3fn_x4", "uint8"
+POW = [1, 2, 3, 4, 8, 12, 16, 32, 48, 64]
+SCRATCH = {}
+
+
+def _sb(dtype, **kw):
+    for k, n in kw.items():
+        SCRATCH[k] = ("sbuf", [128, n], dtype)
+
+
+_sb(I4, nxi=20, rnx=20, jp=C, jpa=C, jm=C, pc=20, c16=20, pa=20, idi=20, di=40, da=40)
+_sb(BF, xin=4 * C, ut=512, vt=512, xt=4 * C, zt=4 * C, tb=4 * C, tp=4 * C, hb=4 * C, gb=4 * C, zb=4 * C,
+    M=C, rst=C, iotac=C, zero=2 * C, low0=48, low1=48, og=48, ones=516, ef=516, rk=len(POW) * C, pm0=C, pm1=C, sc0=C, sc1=C,
+    hr=C, posr=C, ordr=C, uu=C, sg=C, svc=C, gsv=C, lvs=C, d3=C, th3=16, vf=2 * C, nvf=2 * C, cb=656)
+_sb(F4, jf=C, jS=C, KE=C, KO=C, M20=C, ov=2, of=3, nb=2, thr=1, lv=20, pos2=20, dq=20, ph2=20, t1=20, t2=20,
+    gS=C, cap=2 * C, fi=1296, wr=2, xm=2 * C, xsc=2 * C, rst2=2 * C, nrr=C, yo=C)
+_sb(U2, lk=60, ou=2, ou1=2, ol=20, gl=20, hl=20, ql=20, pu=20, idl=20, ul=8)
+for _r in range(3):
+    _sb(U2, **{"lab%d" % _r: 40, "rlab%d" % _r: 40})
+    _sb(CO, **{"rq%d" % _r: C})
+    _sb(PL, **{"rs%d" % _r: C})
+    if _r: _sb(U2, **{"glab%d" % _r: 40})
+for _r in range(4):
+    _sb(CO, **{"xq%d" % _r: C})
+    _sb(PL, **{"xs%d" % _r: C})
+_sb(CO, zq=C, uq=128, uw=128, vq=128, wq=512, eq=512)
+_sb(PL, zs=C, us=128, uws=128, vs=128, wsb=512, es=512)
+for _r in range(8):
+    SCRATCH["ps%d" % _r] = ("psum", [128, 512], F4)
+SEMAPHORES = ["cv", "ct", "ca", "cg", "d_nx", "d_x", "d_u", "d_wc", "d_ws", "d_v", "d_out", "sent", "r_nx"] + \
+    ["r_x%d" % r for r in range(3)] + ["r_l%d" % r for r in range(3)] + ["r_g%d" % r for r in (1, 2)]
+
+
+def rank_program(g, core, T, topo):
+    rank = T.rank_of(core)
+    if rank is None:
+        return
+    A, ACT = AluOpType, ActivationFunctionType
+    ve, te, sc, sy = g.vector, g.tensor, g.scalar, g.sync
+    Q = {"v": ve, "t": te, "a": sc, "g": g, "s": sy}
+    count = {}
+    clock = {q: {} for q in Q}
+    wrote, read = {}, {}
+
+    def need(q, tok):
+        name, val, snap = tok
+        if clock[q].get(name, 0) < val:
+            Q[q].wait_ge(T.sem[name], val)
+            for k, v in list(snap.items()) + [(name, val)]:
+                clock[q][k] = max(clock[q].get(k, 0), v)
+
+    def waits(q, rd, wr):
+        toks = [wrote[k] for k in rd]
+        for k in wr:
+            if k in wrote: toks.append(wrote[k])
+            toks += read.get(k, [])
+        best = {}
+        for t in toks:
+            if t[0] not in best or best[t[0]][1] < t[1]: best[t[0]] = t
+        for t in best.values(): need(q, t)
+
+    def op(q, fn, rd, wr, sem=None, inc=1):
+        rd, wr = rd.split(), wr.split()
+        waits(q, rd, wr)
+        sem = sem or "c" + q
+        count[sem] = count.get(sem, 0) + inc
+        fn().then_inc(T.sem[sem], inc)
+        tok = (sem, count[sem], dict(clock[q]))
+        for k in rd: read.setdefault(k, []).append(tok)
+        for k in wr: wrote[k], read[k] = tok, []
+        return tok
+
+    def dma(q, out, in_, sem, rd, wr):
+        return op(q, lambda: Q[q].dma_start(out, in_), rd, wr, sem, 16)
+
+    def send(dst, pieces, rsem, rd):
+        waits("g", rd.split(), [])
+        rid, pid = topo.addr(dst, core)
+        mask, n = topo.mask(core, dst), len(topo.engines(core, dst))
+        for out, in_ in pieces:
+            g.remote_dma(out, in_, T.sem[rsem], T.sem.sent, pid, rid, mask)
+            count["sent"] = count.get("sent", 0) + n
+            count[rsem] = count.get(rsem, 0) + n
+
+    def landed(rsem, val, wr):
+        for k in wr.split(): wrote[k] = (rsem, val, {})
+
+    partner = [T.cores[rank ^ m] for m in MASK]
+    NE = len(topo.engines(core, partner[0]))
+    TT = lambda out, a, b, o, rd, wr: op("v", lambda: ve.tensor_tensor(out, a, b, o), rd, wr)
+    TS = lambda out, a, s1, s2, o, o2, rd, wr: op("v", (lambda: ve.tensor_scalar(out, a, s1, s2, o, o2)) if o2 is not None else (lambda: ve.tensor_scalar(out, a, s1, None, o)), rd, wr)
+    TC = lambda out, a, rd, wr: op("v", lambda: ve.tensor_copy(out, a), rd, wr)
+    SCAN = lambda out, a, b, i, o, o2, rd, wr: op("v", lambda: ve.tensor_tensor_scan(out, a, b, i, o, o2), rd, wr)
+    MS = lambda ap, c, wr: op("v", lambda: ve.memset(ap, c), "", wr)
+    AC = lambda out, a, rd, wr, scale=1.0: op("a", lambda: sc.activation(out, a, ACT.Copy, scale=scale), rd, wr)
+    ID = lambda out, a, bias, scale, rd, wr: op("a", lambda: sc.activation(out, a, ACT.Identity, bias=bias, scale=scale), rd, wr)
+    QZ = lambda q, s, t, rd, wr: op("v", lambda: ve.quantize_mx(q, s, t), rd, wr)
+    MM = lambda ps, l, ls, m, ms, rd, wr: op("t", lambda: te.matmul_mx(ps, l, ls, m, ms, True, True), rd, wr)
+    PLN = lambda buf, b: buf[:, C * b:C * b + C]
+    turn = [0]
+
+    dma("s", T.nxi[:, :], T.nx[:, :], "d_nx", "", "nxi")
+    dma("s", T.xin[:, :], T.x[:, :], "d_x", "", "xin")
+    dma("s", T.ut[:, :], T.u[:, :], "d_u", "", "ut")
+    dma("s", T.wq[:, :].bitcast(dt.uint8), T.wc[:, :], "d_wc", "", "wq")
+    dma("s", T.wsb[:, :], T.ws[:, :], "d_ws", "", "wsb")
+    dma("s", T.vt[:, :], T.v[:, :], "d_v", "", "vt")
+
+    op("g", lambda: g.iota(T.jp[:, :], [[0, 20], [1, 16]], 0, -1), "", "jp")
+    op("g", lambda: g.iota(T.jm[:, :], [[0, 20], [1, 16]], 0, 0), "", "jm")
+    op("g", lambda: g.iota(T.iotac[:, :], [[1, C]], -160, 0, allow_small_or_imprecise_dtypes=True), "", "iotac")
+    send(partner[0], [(T.rnx[:, :], T.nxi[:, :])], "r_nx", "nxi")
+    landed("r_nx", NE, "rnx")
+    op("g", lambda: g.iota(T.pc[:, :], [[0, 20]], 0, 1), "", "pc")
+    op("g", lambda: g.iota(T.c16[:, :], [[16, 20]], 0, 0), "", "c16")
+    MS(T.ones[:, :], 1.0, "ones")
+    op("g", lambda: g.affine_select(T.ef[:, :], T.ones[:, :], [[-1, 516]], A.is_equal, 0.0, 3, 4), "ones", "ef")
+    op("g", lambda: g.iota(T.jf[:, :], [[1, C]], 0, 0, allow_small_or_imprecise_dtypes=True), "", "jf")
+    MS(T.of[:, 0:1], -160.0, "of0")
+    MS(T.ou[:, :], 0, "ou")
+    MS(T.low0[:, :], 0.0, "low0")
+    MS(T.low1[:, :], 0.0, "low1")
+    TS(T.jpa[:, :], T.jp[:, :], 15, None, A.bitwise_and, None, "jp", "jpa")
+    TS(T.M[:, :], T.jpa[:, :], 0.0, None, A.is_equal, None, "jpa", "M")
+    TS(T.rst[:, :], T.jm[:, :], 0.0, None, A.is_gt, None, "jm", "rst")
+
+    fillers = []
+
+    def gap(n=1):
+        for _ in range(n):
+            if fillers: fillers.pop(0)()
+
+    def conv(pieces, finish):
+        b = turn[0] = 1 - turn[0]
+        pm, s, kp, ks = T["pm%d" % b], T["sc%d" % b], "pm%d" % b, "sc%d" % b
+        at, keys = 0, []
+        for i, (win, off, rd, n) in enumerate(pieces):
+            k = kp if i == 0 else "%s_%d" % (kp, i)
+            TT(pm[:, at:at + n], win.indirect(off), T.M[:, 0:n], A.mult, rd + " M", kp if i == 0 else k)
+            keys.append(k)
+            at += n
+        gap()
+        SCAN(s[:, 0:at], T.rst[:, 0:at], pm[:, 0:at], 0.0, A.mult, A.add, " ".join(keys) + " rst", ks)
+        gap()
+        finish(s[:, 15:at:16], ks)
+        gap()
+
+    def to_list(out, wr):
+        return lambda v, k: TS(out, v, 160.0, None, A.add, None, k, wr)
+
+    RK = {m: T.rk[:, C * i:C * i + C] for i, m in enumerate(POW)}
+    LK = {m: T.lk[:, 20 * i:20 * i + 20] for i, m in enumerate([1, 4, 16])}
+    IDL, OLALL = T.idl[:, :], "ol0 ol1 ol2 ol3 ol4 ol5 ol6 ol7"
+
+    def times(m, by):
+        AC(RK[m + by], RK[m].indirect(LK[by]), "rk%d lk%d" % (m, by), "rk%d" % (m + by))
+
+    def listed(m, by):
+        conv([(RK[m], LK[by], "rk%d lk%d" % (m, by), C)], to_list(LK[m + by], "lk%d" % (m + by)))
+
+    def digit(l, d, m, lst, k):
+        TT(T.og[:, 16 * d - 16:16 * d], RK[m].indirect(lst), T["low%d" % l][:, 16 * d - 16:16 * d], A.mult, "rk%d low%d " % (m, l) + k, "og%d" % d)
+
+    def digits(l, out, wr):
+        op("v", lambda: ve.tensor_reduce(T.ov[:, l:l + 1], T.og[:, :], AxisListType.X, A.add), "og1 og2 og3", "ov%d" % l)
+        gap()
+        TS(T.of[:, l + 1:l + 2], T.of[:, l:l + 1], T.nb[:, l:l + 1], T.ov[:, l:l + 1], A.mult, A.add, "of%d nb%d ov%d" % (l, l, l), "of%d" % (l + 1))
+        gap()
+        TS(out, T.of[:, l + 1:l + 2], 160.0, None, A.add, None, "of%d" % (l + 1), wr)
+
+    def xname(r): return T["xq%d" % r], T["xs%d" % r], "xq%d" % r
+
+    def quant_x(r):
+        q, s, k = xname(r)
+        t, tk = (T.xin, "xin") if r == 0 else (T.xt, "xt0 xt1 xt2 xt3")
+        QZ(q[:, :], s[:, :], t[:, :], tk, k)
+
+    def quant_e(b):
+        QZ(T.eq[:, 128 * b:128 * b + 128], T.es[:, 128 * b:128 * b + 128], T.ef[:, 3 - b:515 - b], "ef", "eq%d" % b)
+
+    def spread(r, q, s, k, banks):
+        for b in range(4):
+            MM(T["ps%d" % banks[b]][:, 0:C], T.eq[:, 128 * b:128 * b + 128], T.es[:, 128 * b:128 * b + 128], q[:, :], s[:, :], "eq%d " % b + k, "ps%d" % banks[b])
+
+    NEAR, FAR = [1, 2, 3, 4], [5, 6, 7, 0]
+
+    def start(r):
+        q, s, k = xname(r)
+        send(partner[r], [(T["rq%d" % r][:, :].bitcast(dt.uint8), q[:, :].bitcast(dt.uint8)), (T["rs%d" % r][:, :], s[:, :])], "r_x%d" % r, k)
+        landed("r_x%d" % r, 2 * NE, "rq%d" % r)
+
+    def scores(r):
+        q, s, k = xname(r)
+        for p in (0, 7):
+            MM(T["ps%d" % p][:, 0:C], T.uw[:, :], T.uws[:, :], q[:, :], s[:, :], "uw " + k, "ps%d" % p)
+
+    def unpack(b):
+        AC(PLN(T.tb, b), T["ps%d" % NEAR[b]][:, 0:C], "ps%d" % NEAR[b], "tb%d" % b, 0.5)
+
+    def unpack_far(r):
+        q, s, k = T["rq%d" % r], T["rs%d" % r], "rq%d" % r
+        spread(r, q, s, k, FAR)
+        for b in range(4):
+            AC(PLN(T.tp, b), T["ps%d" % FAR[b]][:, 0:C], "ps%d" % FAR[b], "tp%d" % b, 0.5)
+
+    def guests(r):
+        if r == 0: return T.gl[:, :], T.hl[:, :], "gl", "hl"
+        return T["glab%d" % r][:, 0:20], T["glab%d" % r][:, 20:40], "glab%d" % r, "glab%d" % r
+
+    def f_u(r):
+        TS(T.uu[:, :], T.ps0[:, 0:C], 0.0, None, A.is_gt, None, "ps0", "uu")
+        op("a", lambda: sc.activation(T.sg[:, :], T.ps7[:, 0:C], ACT.Sign), "ps7", "sg")
+
+    def f_sv(r):
+        gL, hL, gk, hk = guests(r)
+        TT(T.svc[:, :], T.uu[:, :].indirect(hL), T.sg[:, :], A.is_ge, "uu sg " + hk, "svc")
+
+    def f_lv():
+        SCAN(T.lvs[:, :], T.d3[:, :], T.svc[:, :], 0.0, A.mult, A.add, "svc d3", "lvs")
+        TS(T.lv[:, :], T.lvs[:, 15:C:16], T.thr[:, 0:1], None, A.is_lt, None, "lvs thr", "lv")
+
+    TC(LK[1], T.nxi[:, :], "nxi", "lk1")
+    AC(RK[1], T.iotac[:, :].indirect(LK[1]), "iotac lk1", "rk1")
+    for d in range(1, 4):
+        TC(T.low0[:, 16 * d - 16 + d:16 * d:4], T.M[:, d:16:4], "M", "low0")
+        TC(T.low1[:, 16 * d - 16 + 4 * d:16 * d - 12 + 4 * d], T.M[:, 4 * d:4 * d + 4], "M", "low1")
+    op("v", lambda: ve.tensor_reduce(T.nb[:, 0:1], T.M[:, 0:16:4], AxisListType.X, A.add), "M", "nb0")
+    op("v", lambda: ve.tensor_reduce(T.nb[:, 1:2], T.M[:, 0:4], AxisListType.X, A.add), "M", "nb1")
+    times(1, 1); times(2, 1); times(3, 1)
+    digit(0, 1, 1, T.ou[:, 0:1], "ou")
+    TS(T.pa[:, :], T.pc[:, :], 15, None, A.bitwise_and, None, "pc", "pa")
+    TT(T.idi[:, :], T.pa[:, :], T.c16[:, :], A.add, "pa c16", "idi")
+    MS(T.cb[:, 0:1], -160.0, "cb0")
+    TC(T.idl[:, :], T.idi[:, :], "idi", "idl")
+    digit(0, 2, 2, T.ou[:, 0:1], "ou")
+    TS(T.d3[:, :], T.M[:, :], -3.0, 3.0, A.mult, A.add, "M", "d3")
+    fillers += [lambda: digit(0, 3, 3, T.ou[:, 0:1], "ou"),
+                lambda: TC(T.ul[:, :], T.c16[:, 0:8], "c16", "ul"),
+                lambda: MS(T.fi[:, 0:1], 0.0, "fi0")]
+    listed(3, 1)
+    times(4, 4); times(8, 4); times(12, 4)
+    fillers += [lambda: SCAN(T.th3[:, :], T.d3[:, 0:16], T.M[:, 0:16], 0.0, A.mult, A.add, "d3 M", "th3"),
+                lambda: MS(T.fi[:, 1287:1288], 1.0, "fi1")]
+    digits(0, T.ou1[:, 0:1], "ou1")
+    TS(T.thr[:, :], T.th3[:, 15:16], 0.75, None, A.mult, None, "th3", "thr")
+    digit(1, 1, 4, T.ou1[:, 0:1], "ou1")
+    quant_x(0)
+    start(0)
+    digit(1, 2, 8, T.ou1[:, 0:1], "ou1")
+    QZ(T.uq[:, :], T.us[:, :], T.ut[:, :], "ut", "uq")
+    fillers += [lambda: digit(1, 3, 12, T.ou1[:, 0:1], "ou1"),
+                lambda: TC(T.uw[:, :].bitcast(dt.uint32), T.uq[:, :].bitcast(dt.uint32).indirect(T.ul[:, :]), "uq ul", "uwc"),
+                lambda: TC(T.uws[:, :], T.us[:, :].indirect(T.ul[:, :]), "uq ul uwc", "uw")]
+    listed(12, 4)
+    scores(0)
+    times(16, 16); times(32, 16); times(48, 16)
+    fillers += [lambda: TC(T.gl[:, :], T.rnx[:, :], "rnx", "gl"), lambda: MS(T.zero[:, :], 0.0, "zero")]
+    digits(1, T.ol[:, 0:1], "ol0")
+    for b in range(4): quant_e(b)
+    spread(0, T.xq0, T.xs0, "xq0", NEAR)
+    S20 = 2.0 ** -20
+    AC(T.jS[:, :], T.jf[:, :], "jf", "jS", S20)
+    ID(T.KE[:, :], T.jf[:, :], 641 * 512 * S20, 1024 * S20, "jf", "KE")
+    ID(T.KO[:, :], T.jf[:, :], 642 * 512 * S20, 1024 * S20, "jf", "KO")
+    AC(T.M20[:, :], T.M[:, :], "M", "M20", 2.0 ** 20)
+    AC(T.rst2[:, 0:C], T.rst[:, :], "rst", "rst2a")
+    AC(T.rst2[:, C:], T.rst[:, :], "rst", "rst2b")
+    op("v", lambda: ve.tensor_copy(T.hr[:, :].indirect(T.gl[:, :]), T.iotac[:, :]), "gl iotac", "hr")
+    conv([(RK[16 * d], T.ol[:, 0:1], "rk%d ol0" % (16 * d), 16) for d in range(1, 4)], to_list(T.ol[:, 1:4], "ol1"))
+    for i in range(4):
+        if i == 0: fillers += [lambda: f_u(0)]
+        if i == 1: conv([(T.hr[:, :], IDL, "hr idl", C)], to_list(T.hl[:, :], "hl"))
+        if i == 2: fillers += [lambda: f_sv(0)]
+        if i == 3: fillers += [lambda: f_lv()]
+        conv([(RK[64], T.ol[:, 4 * i:4 * i + 4], "rk64 " + ("ol0 ol1" if i == 0 else "ol%d" % (i + 1)), 64)], to_list(T.ol[:, 4 * i + 4:4 * i + 8], "ol%d" % (i + 2)))
+    gap(len(fillers))
+    OLALL = "ol0 ol1 ol2 ol3 ol4 ol5"
+
+    def slots(r):
+        gL, hL, gk, hk = guests(r)
+        AC(T.gsv[:, :], T.svc[:, :].indirect(gL), "svc " + gk, "gsv")
+        AC(T.vf[:, 0:2 * C:2], T.svc[:, :].indirect(T.ol[:, :]), "svc " + OLALL, "vfa")
+        ID(T.vf[:, 1:2 * C:2], T.gsv[:, :].indirect(T.ol[:, :]), 1.0, -1.0, "gsv " + OLALL, "vfb")
+        ID(T.nvf[:, :], T.vf[:, :], 1.0, -1.0, "vfa vfb", "nvf")
+
+    def cap_even(): TT(T.cap[:, 0:2 * C:2], T.jS[:, :].indirect(T.ol[:, :]), T.KE[:, :], A.add, "jS KE " + OLALL, "capa")
+
+    def cap_odd(): TT(T.cap[:, 1:2 * C:2], T.gS[:, :].indirect(T.ol[:, :]), T.KO[:, :], A.add, "gS KO " + OLALL, "capb")
+
+    def guest_cols(r):
+        gL, hL, gk, hk = guests(r)
+        AC(T.gS[:, :], T.jS[:, :].indirect(gL), "jS " + gk, "gS")
+
+    def host_place(r):
+        gL, hL, gk, hk = guests(r)
+
+        def fin(v, k):
+            TS(T.ph2[:, :], v, 2.0, 321.0, A.mult, A.add, k, "ph2")
+            TT(T.dq[:, :], T.ph2[:, :], T.pos2[:, :], A.subtract, "ph2 pos2", "dq")
+        conv([(T.posr[:, :], hL, "posr " + hk, C)], fin)
+
+    slots(0)
+    guest_cols(0)
+    for b in range(4): unpack(b)
+    op("v", lambda: ve.tensor_copy(T.posr[:, :].indirect(T.ol[:, :]), T.iotac[:, :]), "iotac " + OLALL, "posr")
+    fillers += [cap_even]
+    conv([(T.posr[:, :], IDL, "posr idl", C)], lambda v, k: TS(T.pos2[:, :], v, 2.0, 320.0, A.mult, A.add, k, "pos2"))
+    fillers += [cap_odd]
+    host_place(0)
+
+    for r in range(3):
+        lab, rlab, lk, rk = T["lab%d" % r], T["rlab%d" % r], "lab%d" % r, "rlab%d" % r
+        last = r == 2
+        if r:
+            quant_x(r)
+            start(r)
+            scores(r)
+            q, s, k = xname(r)
+            spread(r, q, s, k, NEAR)
+            cap_even()
+            f_u(r)
+            unpack(0)
+            f_sv(r)
+            slots(r)
+            f_lv()
+            fillers += [cap_odd]
+            host_place(r)
+            unpack(1); unpack(2); unpack(3)
+        unpack_far(r)
+        TT(T.t1[:, :], T.lv[:, :], T.dq[:, :], A.mult, "lv dq", "t1")
+        TT(T.t2[:, :], T.t1[:, :], T.pos2[:, :], A.add, "t1 pos2", "t2")
+        SCAN(T.fi[:, 1:641], T.vf[:, :], T.cap[:, :], 0.0, A.max, A.min, "vfa vfb capa capb", "fif")
+        TC(T.ql[:, :], T.t2[:, :], "t2", "ql")
+        SCAN(T.fi[:, 1286:646:-1], T.nvf[:, ::-1], T.cap[:, ::-1], 1.0, A.min, A.max, "nvf capa capb", "fib")
+        TT(T.xm[:, C:], T.fi[:, 0:640].indirect(T.ql[:, :]), T.M20[:, :], A.mult, "fif fi0 ql M20", "xmb")
+        TT(T.xm[:, 0:C], T.fi[:, 648:1288].indirect(T.ql[:, :]), T.M20[:, :], A.mult, "fib fi1 ql M20", "xma")
+        TS(T.wr[:, :], T.fi[:, 640:648:7], 2.0 ** 20, None, A.mult, None, "fif fib", "wr")
+        SCAN(T.xsc[:, :], T.rst2[:, :], T.xm[:, :], 0.0, A.mult, A.add, "rst2a rst2b xma xmb", "xsc")
+        TS(T.di[:, 0:20], T.xsc[:, 15:C:16], -327680.0, T.wr[:, 1:2], A.add, A.min, "xsc wr", "dia")
+        TS(T.di[:, 20:40], T.xsc[:, C + 15:2 * C:16], 327680.0, T.wr[:, 0:1], A.add, A.max, "xsc wr", "dib")
+        TS(T.da[:, :], T.di[:, :], 511, None, A.bitwise_and, None, "dia dib", "da")
+        TC(lab[:, :], T.da[:, :], "da", lk)
+        send(partner[r], [(rlab[:, :], lab[:, :])], "r_l%d" % r, lk)
+        landed("r_l%d" % r, NE, rk)
+        if not last:
+            n = r + 1
+            send(partner[n], [(T["glab%d" % n][:, :], lab[:, :])], "r_g%d" % n, lk)
+            landed("r_g%d" % n, NE, "glab%d" % n)
+        a, b_, ra, rb = lab[:, 0:20], lab[:, 20:40], rlab[:, 0:20], rlab[:, 20:40]
+        for b in range(4):
+            AC(PLN(T.gb, b), PLN(T.tb, b).indirect(b_), "tb%d " % b + lk, "gb%d" % b)
+        if not last:
+            SCAN(T.cb[:, 1:641], T.vf[:, :], T.zero[:, :], -160.0, A.add, A.add, "vfa vfb zero", "cb")
+
+            def fin(v, k):
+                TS(T.pu[:, :], v, 160.0, None, A.add, None, k, "pu")
+                TS(T.pos2[:, :], v, 2.0, 320.0, A.mult, A.add, k, "pos2")
+            conv([(T.cb[:, 0:640], T.ql[:, :], "cb cb0 ql", C)], fin)
+            op("v", lambda: ve.tensor_copy(T.ordr[:, :].indirect(T.pu[:, :]), T.iotac[:, :]), "pu iotac", "ordr")
+        else:
+            QZ(T.vq[:, :], T.vs[:, :], T.vt[:, :], "vt", "vq")
+        AC(T.zb[:, 0:160], PLN(T.tp, 0).indirect(rlab[:, 20:30]), "tp0 " + rk, "zb0a")
+        TC(T.zb[:, 160:C], PLN(T.tp, 0).indirect(rlab[:, 30:40]), "tp0 " + rk, "zb0")
+        for b in range(1, 4):
+            AC(PLN(T.zb, b), PLN(T.tp, b).indirect(rb), "tp%d " % b + rk, "zb%d" % b)
+        for b in range(4):
+            TT(T.zt[:, b:4 * C:4], PLN(T.tp, b).indirect(ra), PLN(T.zb, b), A.add, "tp%d zb%d " % (b, b) + rk + (" zb0a" if b == 0 else ""), "zt%d" % b)
+        QZ(T.zq[:, :], T.zs[:, :], T.zt[:, :], "zt0 zt1 zt2 zt3", "zq")
+        for b in range(4):
+            MM(T["ps%d" % (b + 1)][:, 0:C], T.wq[:, 128 * b:128 * b + 128], T.wsb[:, 128 * b:128 * b + 128], T.zq[:, :], T.zs[:, :], "wq wsb zq", "ps%d" % (b + 1))
+        if not last:
+            AC(T.posr[:, :], T.cb[:, 0:640].indirect(T.ql[:, :]), "cb cb0 ql", "posr")
+            conv([(T.ordr[:, :], IDL, "ordr idl", C)], to_list(T.ol[:, :], OLALL))
+        for b in range(4):
+            AC(PLN(T.hb, b), T["ps%d" % (b + 1)][:, 0:C], "ps%d" % (b + 1), "hb%d" % b, 2.0 ** -6)
+        for b in range(4):
+            TT(T.xt[:, b:4 * C:4], PLN(T.hb, b).indirect(a), PLN(T.gb, b), A.add, "hb%d gb%d " % (b, b) + lk, "xt%d" % b)
+        if not last:
+            guest_cols(r + 1)
+        else:
+            AC(T.nrr[:, :], T.jf[:, :].indirect(a), "jf " + lk, "nrr")
+            dma("s", T.nr[:, :], T.nrr[0:128:16, :], "d_out", "nrr", "nr")
+
+    q, s, k = xname(3)
+    quant_x(3)
+    MM(T.ps0[:, 0:C], T.vq[:, :], T.vs[:, :], q[:, :], s[:, :], "vq " + k, "ps0")
+    dma("s", T.oc[:, :], q[:, :].bitcast(dt.uint8), "d_out", k, "oc")
+    for i in range(4):
+        dma("a" if i % 2 else "s", T.osc[4 * i:4 * i + 4, :], s[32 * i:32 * i + 4, :], "d_out", k, "osc%d" % i)
+    TC(T.yo[:, :], T.ps0[:, 0:C], "ps0", "yo")
+    dma("s", T.y[:, :], T.yo[:, :], "d_out", "yo", "y")
+    for name in SEMAPHORES:
+        if count.get(name): need("s", (name, count[name], {}))

@@ -1,7 +1,7 @@
 from concourse.mybir import dt, AluOpType, AxisListType, ActivationFunctionType
 
 N, C, MASK = 8, 320, [4, 1, 2]
-BF, F4, F2, I4, U2, CO, PL = "bfloat16", "float32", "float16", "int32", "uint16", "float8_e4m3fn_x4", "uint8"
+BF, F4, I4, U2, CO, PL = "bfloat16", "float32", "int32", "uint16", "float8_e4m3fn_x4", "uint8"
 POW = [1, 2, 3, 4, 8, 12, 16, 32, 48, 64]
 SCRATCH = {}
 
@@ -11,13 +11,13 @@ def _sb(dtype, **kw):
         SCRATCH[k] = ("sbuf", [128, n], dtype)
 
 
-_sb(I4, nxi=20, rnx=20, jp=C, jpa=C, jm=C, pc=20, c16=20, pa=20, idi=20, di=40, da=40)
+_sb(I4, nxi=20, rnx=20, jp=C, jpa=C, c16=8, di=40, da=40)
 _sb(BF, xin=4 * C, ut=512, vt=512, xt=4 * C, zt=4 * C, tb=4 * C, tp=4 * C, hb=4 * C, gb=4 * C, zb=4 * C,
     M=C, rst=C, iotac=C, zero=2 * C, low0=48, low1=48, og=48, ones=516, ef=516, rk=len(POW) * C, pm0=C, pm1=C, sc0=C, sc1=C,
-    hr=C, posr=C, ordr=C, uu=C, sg=C, svc=C, gsv=C, lvs=C, d3=C, th3=16, vf=2 * C, nvf=2 * C, cb=656)
-_sb(F4, jf=C, jS=C, KE=C, KO=C, M20=C, ov=2, of=3, nb=2, thr=1, lv=20, pos2=20, dq=20, ph2=20, t1=20, t2=20,
+    hr=C, posr=C, ordr=C, uu=C, sg=C, svc=C, gsv=C, lvs=C, d3=C, th3=16, dR=C, iotaT=C, phr=C, vf=2 * C, nvf=2 * C, cb=656)
+_sb(F4, dI=16, mP=16, wn=16, wn2=1, wc0=C, wc1=C, jf=C, jS=C, KE=C, KO=C, M20=C, ov=2, of=3, nb=2, thr=1, lv=20, pos2=20, dq=20, ph2=20, t1=20, t2=20,
     gS=C, cap=2 * C, fi=1296, wr=2, xm=2 * C, xsc=2 * C, rst2=2 * C, nrr=C, yo=C)
-_sb(U2, lk=60, ou=2, ou1=2, ol=20, gl=20, hl=20, ql=20, pu=20, idl=20, ul=8)
+_sb(U2, lk=60, ou=2, ou1=2, ol=20, gl=20, hl=20, ql=20, pu=20, ul=8)
 for _r in range(3):
     _sb(U2, **{"lab%d" % _r: 40, "rlab%d" % _r: 40})
     _sb(CO, **{"rq%d" % _r: C})
@@ -110,22 +110,22 @@ def rank_program(g, core, T, topo):
     dma("s", T.vt[:, :], T.v[:, :], "d_v", "", "vt")
 
     op("g", lambda: g.iota(T.jp[:, :], [[0, 20], [1, 16]], 0, -1), "", "jp")
-    op("g", lambda: g.iota(T.jm[:, :], [[0, 20], [1, 16]], 0, 0), "", "jm")
     op("g", lambda: g.iota(T.iotac[:, :], [[1, C]], -160, 0, allow_small_or_imprecise_dtypes=True), "", "iotac")
     send(partner[0], [(T.rnx[:, :], T.nxi[:, :])], "r_nx", "nxi")
     landed("r_nx", NE, "rnx")
-    op("g", lambda: g.iota(T.pc[:, :], [[0, 20]], 0, 1), "", "pc")
-    op("g", lambda: g.iota(T.c16[:, :], [[16, 20]], 0, 0), "", "c16")
     MS(T.ones[:, :], 1.0, "ones")
     op("g", lambda: g.affine_select(T.ef[:, :], T.ones[:, :], [[-1, 516]], A.is_equal, 0.0, 3, 4), "ones", "ef")
+    op("g", lambda: g.iota(T.c16[:, :], [[16, 8]], 0, 0), "", "c16")
+    MS(T.rst[:, :], 1.0, "rst")
+    MS(T.rst[:, 0:C:16], 0.0, "rst")
     op("g", lambda: g.iota(T.jf[:, :], [[1, C]], 0, 0, allow_small_or_imprecise_dtypes=True), "", "jf")
-    MS(T.of[:, 0:1], -160.0, "of0")
+    MS(T.of[:, 0:1], -160.0 * 2.0 ** -96, "of0")
     MS(T.ou[:, :], 0, "ou")
+    MS(T.zero[:, :], 0.0, "zero")
     MS(T.low0[:, :], 0.0, "low0")
     MS(T.low1[:, :], 0.0, "low1")
     TS(T.jpa[:, :], T.jp[:, :], 15, None, A.bitwise_and, None, "jp", "jpa")
     TS(T.M[:, :], T.jpa[:, :], 0.0, None, A.is_equal, None, "jpa", "M")
-    TS(T.rst[:, :], T.jm[:, :], 0.0, None, A.is_gt, None, "jm", "rst")
 
     fillers = []
 
@@ -148,18 +148,31 @@ def rank_program(g, core, T, topo):
         finish(s[:, 15:at:16], ks)
         gap()
 
+    S96, P96 = 2.0 ** -96, 2.0 ** 96
+
     def to_list(out, wr):
-        return lambda v, k: TS(out, v, 160.0, None, A.add, None, k, wr)
+        return lambda v, k: TS(out, v, P96, 160.0, A.mult, A.add, k, wr)
+
+    def weigh(src, rd, finish):
+        b = turn[0] = 1 - turn[0]
+        w, k = T["wc%d" % b], "wc%d" % b
+        SCAN(w[:, :], T.dR[:, :], src, 0.0, A.mult, A.add, rd + " dR", k)
+        gap()
+        finish(w[:, 15:C:16], k)
+        gap()
+
+    def to_wlist(out, wr):
+        return lambda v, k: TS(out, v, T.wn[:, 15:16], 160.0, A.mult, A.add, k + " wn", wr)
 
     RK = {m: T.rk[:, C * i:C * i + C] for i, m in enumerate(POW)}
     LK = {m: T.lk[:, 20 * i:20 * i + 20] for i, m in enumerate([1, 4, 16])}
-    IDL, OLALL = T.idl[:, :], "ol0 ol1 ol2 ol3 ol4 ol5 ol6 ol7"
+    OLALL = "ol0 ol1 ol2 ol3 ol4 ol5"
 
     def times(m, by):
         AC(RK[m + by], RK[m].indirect(LK[by]), "rk%d lk%d" % (m, by), "rk%d" % (m + by))
 
-    def listed(m, by):
-        conv([(RK[m], LK[by], "rk%d lk%d" % (m, by), C)], to_list(LK[m + by], "lk%d" % (m + by)))
+    def listed(m):
+        weigh(RK[m], "rk%d" % m, to_wlist(LK[m], "lk%d" % m))
 
     def digit(l, d, m, lst, k):
         TT(T.og[:, 16 * d - 16:16 * d], RK[m].indirect(lst), T["low%d" % l][:, 16 * d - 16:16 * d], A.mult, "rk%d low%d " % (m, l) + k, "og%d" % d)
@@ -169,7 +182,7 @@ def rank_program(g, core, T, topo):
         gap()
         TS(T.of[:, l + 1:l + 2], T.of[:, l:l + 1], T.nb[:, l:l + 1], T.ov[:, l:l + 1], A.mult, A.add, "of%d nb%d ov%d" % (l, l, l), "of%d" % (l + 1))
         gap()
-        TS(out, T.of[:, l + 1:l + 2], 160.0, None, A.add, None, "of%d" % (l + 1), wr)
+        TS(out, T.of[:, l + 1:l + 2], P96, 160.0, A.mult, A.add, "of%d" % (l + 1), wr)
 
     def xname(r): return T["xq%d" % r], T["xs%d" % r], "xq%d" % r
 
@@ -220,27 +233,33 @@ def rank_program(g, core, T, topo):
 
     def f_lv():
         SCAN(T.lvs[:, :], T.d3[:, :], T.svc[:, :], 0.0, A.mult, A.add, "svc d3", "lvs")
+        gap()
         TS(T.lv[:, :], T.lvs[:, 15:C:16], T.thr[:, 0:1], None, A.is_lt, None, "lvs thr", "lv")
 
     TC(LK[1], T.nxi[:, :], "nxi", "lk1")
-    AC(RK[1], T.iotac[:, :].indirect(LK[1]), "iotac lk1", "rk1")
+    AC(RK[1], T.iotac[:, :].indirect(LK[1]), "iotac lk1", "rk1", S96)
     for d in range(1, 4):
         TC(T.low0[:, 16 * d - 16 + d:16 * d:4], T.M[:, d:16:4], "M", "low0")
         TC(T.low1[:, 16 * d - 16 + 4 * d:16 * d - 12 + 4 * d], T.M[:, 4 * d:4 * d + 4], "M", "low1")
     op("v", lambda: ve.tensor_reduce(T.nb[:, 0:1], T.M[:, 0:16:4], AxisListType.X, A.add), "M", "nb0")
     op("v", lambda: ve.tensor_reduce(T.nb[:, 1:2], T.M[:, 0:4], AxisListType.X, A.add), "M", "nb1")
     times(1, 1); times(2, 1); times(3, 1)
+    AC(T.iotaT[:, :], T.iotac[:, :], "iotac", "iotaT", S96)
+    TS(T.dR[:, :], T.M[:, :], -16384.0, 16384.0, A.mult, A.add, "M", "dR")
+    TS(T.dI[:, :], T.M[:, 0:16], -2.0 ** -14, 2.0 ** -14, A.mult, A.add, "M", "dI")
+    TS(T.mP[:, :], T.M[:, 0:16], P96, None, A.mult, None, "M", "mP")
     digit(0, 1, 1, T.ou[:, 0:1], "ou")
-    TS(T.pa[:, :], T.pc[:, :], 15, None, A.bitwise_and, None, "pc", "pa")
-    TT(T.idi[:, :], T.pa[:, :], T.c16[:, :], A.add, "pa c16", "idi")
+    SCAN(T.wn[:, :], T.dI[:, :], T.mP[:, :], 0.0, A.mult, A.add, "dI mP", "wn")
     MS(T.cb[:, 0:1], -160.0, "cb0")
-    TC(T.idl[:, :], T.idi[:, :], "idi", "idl")
     digit(0, 2, 2, T.ou[:, 0:1], "ou")
+    TS(T.wn2[:, :], T.wn[:, 15:16], 2.0, None, A.mult, None, "wn", "wn2")
     TS(T.d3[:, :], T.M[:, :], -3.0, 3.0, A.mult, A.add, "M", "d3")
-    fillers += [lambda: digit(0, 3, 3, T.ou[:, 0:1], "ou"),
-                lambda: TC(T.ul[:, :], T.c16[:, 0:8], "c16", "ul"),
+    quant_e(0); quant_e(1)
+    digit(0, 3, 3, T.ou[:, 0:1], "ou")
+    quant_e(2); quant_e(3)
+    fillers += [lambda: TC(T.ul[:, :], T.c16[:, :], "c16", "ul"),
                 lambda: MS(T.fi[:, 0:1], 0.0, "fi0")]
-    listed(3, 1)
+    listed(4)
     times(4, 4); times(8, 4); times(12, 4)
     fillers += [lambda: SCAN(T.th3[:, :], T.d3[:, 0:16], T.M[:, 0:16], 0.0, A.mult, A.add, "d3 M", "th3"),
                 lambda: MS(T.fi[:, 1287:1288], 1.0, "fi1")]
@@ -251,39 +270,39 @@ def rank_program(g, core, T, topo):
     start(0)
     digit(1, 2, 8, T.ou1[:, 0:1], "ou1")
     QZ(T.uq[:, :], T.us[:, :], T.ut[:, :], "ut", "uq")
-    fillers += [lambda: digit(1, 3, 12, T.ou1[:, 0:1], "ou1"),
-                lambda: TC(T.uw[:, :].bitcast(dt.uint32), T.uq[:, :].bitcast(dt.uint32).indirect(T.ul[:, :]), "uq ul", "uwc"),
-                lambda: TC(T.uws[:, :], T.us[:, :].indirect(T.ul[:, :]), "uq ul uwc", "uw")]
-    listed(12, 4)
+    TC(T.uw[:, :].bitcast(dt.uint32), T.uq[:, :].bitcast(dt.uint32).indirect(T.ul[:, :]), "uq ul", "uwc")
+    digit(1, 3, 12, T.ou1[:, 0:1], "ou1")
+    op("a", lambda: sc.activation(T.uws[:, :], T.us[:, :].indirect(T.ul[:, :]), ACT.Copy), "uq ul uwc", "uw")
+    listed(16)
     scores(0)
     times(16, 16); times(32, 16); times(48, 16)
-    fillers += [lambda: TC(T.gl[:, :], T.rnx[:, :], "rnx", "gl"), lambda: MS(T.zero[:, :], 0.0, "zero")]
+    fillers += [lambda: TC(T.gl[:, :], T.rnx[:, :], "rnx", "gl")]
     digits(1, T.ol[:, 0:1], "ol0")
-    for b in range(4): quant_e(b)
     spread(0, T.xq0, T.xs0, "xq0", NEAR)
     S20 = 2.0 ** -20
     AC(T.jS[:, :], T.jf[:, :], "jf", "jS", S20)
     ID(T.KE[:, :], T.jf[:, :], 641 * 512 * S20, 1024 * S20, "jf", "KE")
-    ID(T.KO[:, :], T.jf[:, :], 642 * 512 * S20, 1024 * S20, "jf", "KO")
-    AC(T.M20[:, :], T.M[:, :], "M", "M20", 2.0 ** 20)
-    AC(T.rst2[:, 0:C], T.rst[:, :], "rst", "rst2a")
-    AC(T.rst2[:, C:], T.rst[:, :], "rst", "rst2b")
-    op("v", lambda: ve.tensor_copy(T.hr[:, :].indirect(T.gl[:, :]), T.iotac[:, :]), "gl iotac", "hr")
+    op("v", lambda: ve.tensor_copy(T.hr[:, :].indirect(T.gl[:, :]), T.iotaT[:, :]), "gl iotaT", "hr")
     conv([(RK[16 * d], T.ol[:, 0:1], "rk%d ol0" % (16 * d), 16) for d in range(1, 4)], to_list(T.ol[:, 1:4], "ol1"))
     for i in range(4):
         if i == 0: fillers += [lambda: f_u(0)]
-        if i == 1: conv([(T.hr[:, :], IDL, "hr idl", C)], to_list(T.hl[:, :], "hl"))
+        if i == 1: weigh(T.hr[:, :], "hr", to_wlist(T.hl[:, :], "hl"))
+        if i == 1:
+            ID(T.KO[:, :], T.jf[:, :], 642 * 512 * S20, 1024 * S20, "jf", "KO")
+            AC(T.M20[:, :], T.M[:, :], "M", "M20", 2.0 ** 20)
+            AC(T.rst2[:, 0:C], T.rst[:, :], "rst", "rst2a")
         if i == 2: fillers += [lambda: f_sv(0)]
         if i == 3: fillers += [lambda: f_lv()]
         conv([(RK[64], T.ol[:, 4 * i:4 * i + 4], "rk64 " + ("ol0 ol1" if i == 0 else "ol%d" % (i + 1)), 64)], to_list(T.ol[:, 4 * i + 4:4 * i + 8], "ol%d" % (i + 2)))
     gap(len(fillers))
-    OLALL = "ol0 ol1 ol2 ol3 ol4 ol5"
 
     def slots(r):
         gL, hL, gk, hk = guests(r)
         AC(T.gsv[:, :], T.svc[:, :].indirect(gL), "svc " + gk, "gsv")
-        AC(T.vf[:, 0:2 * C:2], T.svc[:, :].indirect(T.ol[:, :]), "svc " + OLALL, "vfa")
+        (TC if r else AC)(T.vf[:, 0:2 * C:2], T.svc[:, :].indirect(T.ol[:, :]), "svc " + OLALL, "vfa")
         ID(T.vf[:, 1:2 * C:2], T.gsv[:, :].indirect(T.ol[:, :]), 1.0, -1.0, "gsv " + OLALL, "vfb")
+
+    def holes():
         ID(T.nvf[:, :], T.vf[:, :], 1.0, -1.0, "vfa vfb", "nvf")
 
     def cap_even(): TT(T.cap[:, 0:2 * C:2], T.jS[:, :].indirect(T.ol[:, :]), T.KE[:, :], A.add, "jS KE " + OLALL, "capa")
@@ -294,22 +313,29 @@ def rank_program(g, core, T, topo):
         gL, hL, gk, hk = guests(r)
         AC(T.gS[:, :], T.jS[:, :].indirect(gL), "jS " + gk, "gS")
 
-    def host_place(r):
+    def host_at(r):
         gL, hL, gk, hk = guests(r)
+        AC(T.phr[:, :], T.posr[:, :].indirect(hL), "posr " + hk, "phr")
+
+    def host_place():
 
         def fin(v, k):
-            TS(T.ph2[:, :], v, 2.0, 321.0, A.mult, A.add, k, "ph2")
+            TS(T.ph2[:, :], v, T.wn2[:, 0:1], 321.0, A.mult, A.add, k + " wn2", "ph2")
+            gap()
             TT(T.dq[:, :], T.ph2[:, :], T.pos2[:, :], A.subtract, "ph2 pos2", "dq")
-        conv([(T.posr[:, :], hL, "posr " + hk, C)], fin)
+        weigh(T.phr[:, :], "phr", fin)
 
     slots(0)
+    op("v", lambda: ve.tensor_copy(T.posr[:, :].indirect(T.ol[:, :]), T.iotaT[:, :]), "iotaT " + OLALL, "posr")
+    host_at(0)
     guest_cols(0)
+    holes()
+    AC(T.rst2[:, C:], T.rst[:, :], "rst", "rst2b")
     for b in range(4): unpack(b)
-    op("v", lambda: ve.tensor_copy(T.posr[:, :].indirect(T.ol[:, :]), T.iotac[:, :]), "iotac " + OLALL, "posr")
     fillers += [cap_even]
-    conv([(T.posr[:, :], IDL, "posr idl", C)], lambda v, k: TS(T.pos2[:, :], v, 2.0, 320.0, A.mult, A.add, k, "pos2"))
+    weigh(T.posr[:, :], "posr", lambda v, k: TS(T.pos2[:, :], v, T.wn2[:, 0:1], 320.0, A.mult, A.add, k + " wn2", "pos2"))
     fillers += [cap_odd]
-    host_place(0)
+    host_place()
 
     for r in range(3):
         lab, rlab, lk, rk = T["lab%d" % r], T["rlab%d" % r], "lab%d" % r, "rlab%d" % r
@@ -325,9 +351,10 @@ def rank_program(g, core, T, topo):
             unpack(0)
             f_sv(r)
             slots(r)
-            f_lv()
+            holes()
             fillers += [cap_odd]
-            host_place(r)
+            f_lv()
+            gap(len(fillers))
             unpack(1); unpack(2); unpack(3)
         unpack_far(r)
         TT(T.t1[:, :], T.lv[:, :], T.dq[:, :], A.mult, "lv dq", "t1")
@@ -350,17 +377,19 @@ def rank_program(g, core, T, topo):
             send(partner[n], [(T["glab%d" % n][:, :], lab[:, :])], "r_g%d" % n, lk)
             landed("r_g%d" % n, NE, "glab%d" % n)
         a, b_, ra, rb = lab[:, 0:20], lab[:, 20:40], rlab[:, 0:20], rlab[:, 20:40]
-        for b in range(4):
-            AC(PLN(T.gb, b), PLN(T.tb, b).indirect(b_), "tb%d " % b + lk, "gb%d" % b)
+        def own_b(b): AC(PLN(T.gb, b), PLN(T.tb, b).indirect(b_), "tb%d " % b + lk, "gb%d" % b)
+
         if not last:
             SCAN(T.cb[:, 1:641], T.vf[:, :], T.zero[:, :], -160.0, A.add, A.add, "vfa vfb zero", "cb")
+            TS(T.posr[:, :], T.cb[:, 0:640].indirect(T.ql[:, :]), S96, None, A.mult, None, "cb cb0 ql", "posr")
 
             def fin(v, k):
-                TS(T.pu[:, :], v, 160.0, None, A.add, None, k, "pu")
-                TS(T.pos2[:, :], v, 2.0, 320.0, A.mult, A.add, k, "pos2")
-            conv([(T.cb[:, 0:640], T.ql[:, :], "cb cb0 ql", C)], fin)
-            op("v", lambda: ve.tensor_copy(T.ordr[:, :].indirect(T.pu[:, :]), T.iotac[:, :]), "pu iotac", "ordr")
-        else:
+                TS(T.pu[:, :], v, T.wn[:, 15:16], 160.0, A.mult, A.add, k + " wn", "pu")
+                TS(T.pos2[:, :], v, T.wn2[:, 0:1], 320.0, A.mult, A.add, k + " wn2", "pos2")
+            weigh(T.posr[:, :], "posr", fin)
+            op("v", lambda: ve.tensor_copy(T.ordr[:, :].indirect(T.pu[:, :]), T.iotaT[:, :]), "pu iotaT", "ordr")
+        for b in range(4): own_b(b)
+        if last:
             QZ(T.vq[:, :], T.vs[:, :], T.vt[:, :], "vt", "vq")
         AC(T.zb[:, 0:160], PLN(T.tp, 0).indirect(rlab[:, 20:30]), "tp0 " + rk, "zb0a")
         TC(T.zb[:, 160:C], PLN(T.tp, 0).indirect(rlab[:, 30:40]), "tp0 " + rk, "zb0")
@@ -372,8 +401,9 @@ def rank_program(g, core, T, topo):
         for b in range(4):
             MM(T["ps%d" % (b + 1)][:, 0:C], T.wq[:, 128 * b:128 * b + 128], T.wsb[:, 128 * b:128 * b + 128], T.zq[:, :], T.zs[:, :], "wq wsb zq", "ps%d" % (b + 1))
         if not last:
-            AC(T.posr[:, :], T.cb[:, 0:640].indirect(T.ql[:, :]), "cb cb0 ql", "posr")
-            conv([(T.ordr[:, :], IDL, "ordr idl", C)], to_list(T.ol[:, :], OLALL))
+            host_at(r + 1)
+            weigh(T.ordr[:, :], "ordr", to_wlist(T.ol[:, :], OLALL))
+            host_place()
         for b in range(4):
             AC(PLN(T.hb, b), T["ps%d" % (b + 1)][:, 0:C], "ps%d" % (b + 1), "hb%d" % b, 2.0 ** -6)
         for b in range(4):

from concourse.mybir import dt, AluOpType, AxisListType, ActivationFunctionType

N, C, MASK = 8, 320, [4, 1, 2]
BF, F4, I4, U2, CO, PL = "bfloat16", "float32", "int32", "uint16", "float8_e4m3fn_x4", "uint8"
POW = [1, 2, 3, 4, 8, 12, 16, 32, 48, 64]
SCRATCH = {}


def _sb(dtype, **kw):
    for k, n in kw.items():
        SCRATCH[k] = ("sbuf", [128, n], dtype)


_sb(I4, nxi=20, rnx=20, jp=C, jpa=C, c16=8, di=40, da=40)
_sb(BF, xin=4 * C, ut=512, vt=512, xt=4 * C, zt=4 * C, tb=4 * C, tp=4 * C, hb=4 * C, gb=4 * C, zb=4 * C,
    M=C, rst=C, iotac=C, zero=2 * C, low0=48, low1=48, og=48, ones=516, ef=516, rk=len(POW) * C, pm0=C, pm1=C, sc0=C, sc1=C,
    hr=C, posr=C, ordr=C, uu=C, sg=C, svc=C, gsv=C, lvs=C, d3=C, th3=16, dR=C, iotaT=C, phr=C, vf=2 * C, nvf=2 * C, cb=656)
_sb(F4, dI=16, mP=16, wn=16, wn2=1, wc0=C, wc1=C, jf=C, jS=C, KE=C, KO=C, M20=C, ov=2, of=3, nb=2, thr=1, lv=20, pos2=20, dq=20, ph2=20, t1=20, t2=20,
    gS=C, cap=2 * C, fi=1296, wr=2, xm=2 * C, xsc=2 * C, rst2=2 * C, nrr=C, yo=C)
_sb(U2, lk=60, ou=2, ou1=2, ol=20, gl=20, hl=20, ql=20, pu=20, ul=8)
for _r in range(3):
    _sb(U2, **{"lab%d" % _r: 40, "rlab%d" % _r: 40})
    _sb(CO, **{"rq%d" % _r: C})
    _sb(PL, **{"rs%d" % _r: C})
    if _r: _sb(U2, **{"glab%d" % _r: 40})
for _r in range(4):
    _sb(CO, **{"xq%d" % _r: C})
    _sb(PL, **{"xs%d" % _r: C})
_sb(CO, zq=C, uq=128, uw=128, vq=128, wq=512, eq=512)
_sb(PL, zs=C, us=128, uws=128, vs=128, wsb=512, es=512)
for _r in range(8):
    SCRATCH["ps%d" % _r] = ("psum", [128, 512], F4)
SEMAPHORES = ["cv", "ct", "ca", "cg", "d_nx", "d_x", "d_u", "d_wc", "d_ws", "d_v", "d_out", "sent", "r_nx"] + \
    ["r_x%d" % r for r in range(3)] + ["r_l%d" % r for r in range(3)] + ["r_g%d" % r for r in (1, 2)]


def rank_program(g, core, T, topo):
    rank = T.rank_of(core)
    if rank is None:
        return
    A, ACT = AluOpType, ActivationFunctionType
    ve, te, sc, sy = g.vector, g.tensor, g.scalar, g.sync
    Q = {"v": ve, "t": te, "a": sc, "g": g, "s": sy}
    count = {}
    clock = {q: {} for q in Q}
    wrote, read = {}, {}

    def need(q, tok):
        name, val, snap = tok
        if clock[q].get(name, 0) < val:
            Q[q].wait_ge(T.sem[name], val)
            for k, v in list(snap.items()) + [(name, val)]:
                clock[q][k] = max(clock[q].get(k, 0), v)

    def waits(q, rd, wr):
        toks = [wrote[k] for k in rd]
        for k in wr:
            if k in wrote: toks.append(wrote[k])
            toks += read.get(k, [])
        best = {}
        for t in toks:
            if t[0] not in best or best[t[0]][1] < t[1]: best[t[0]] = t
        for t in best.values(): need(q, t)

    def op(q, fn, rd, wr, sem=None, inc=1):
        rd, wr = rd.split(), wr.split()
        waits(q, rd, wr)
        sem = sem or "c" + q
        count[sem] = count.get(sem, 0) + inc
        fn().then_inc(T.sem[sem], inc)
        tok = (sem, count[sem], dict(clock[q]))
        for k in rd: read.setdefault(k, []).append(tok)
        for k in wr: wrote[k], read[k] = tok, []
        return tok

    def dma(q, out, in_, sem, rd, wr):
        return op(q, lambda: Q[q].dma_start(out, in_), rd, wr, sem, 16)

    def send(dst, pieces, rsem, rd):
        waits("g", rd.split(), [])
        rid, pid = topo.addr(dst, core)
        mask, n = topo.mask(core, dst), len(topo.engines(core, dst))
        for out, in_ in pieces:
            g.remote_dma(out, in_, T.sem[rsem], T.sem.sent, pid, rid, mask)
            count["sent"] = count.get("sent", 0) + n
            count[rsem] = count.get(rsem, 0) + n

    def landed(rsem, val, wr):
        for k in wr.split(): wrote[k] = (rsem, val, {})

    partner = [T.cores[rank ^ m] for m in MASK]
    NE = len(topo.engines(core, partner[0]))
    TT = lambda out, a, b, o, rd, wr: op("v", lambda: ve.tensor_tensor(out, a, b, o), rd, wr)
    TS = lambda out, a, s1, s2, o, o2, rd, wr: op("v", (lambda: ve.tensor_scalar(out, a, s1, s2, o, o2)) if o2 is not None else (lambda: ve.tensor_scalar(out, a, s1, None, o)), rd, wr)
    TC = lambda out, a, rd, wr: op("v", lambda: ve.tensor_copy(out, a), rd, wr)
    SCAN = lambda out, a, b, i, o, o2, rd, wr: op("v", lambda: ve.tensor_tensor_scan(out, a, b, i, o, o2), rd, wr)
    MS = lambda ap, c, wr: op("v", lambda: ve.memset(ap, c), "", wr)
    AC = lambda out, a, rd, wr, scale=1.0: op("a", lambda: sc.activation(out, a, ACT.Copy, scale=scale), rd, wr)
    ID = lambda out, a, bias, scale, rd, wr: op("a", lambda: sc.activation(out, a, ACT.Identity, bias=bias, scale=scale), rd, wr)
    QZ = lambda q, s, t, rd, wr: op("v", lambda: ve.quantize_mx(q, s, t), rd, wr)
    MM = lambda ps, l, ls, m, ms, rd, wr: op("t", lambda: te.matmul_mx(ps, l, ls, m, ms, True, True), rd, wr)
    PLN = lambda buf, b: buf[:, C * b:C * b + C]
    turn = [0]

    dma("s", T.nxi[:, :], T.nx[:, :], "d_nx", "", "nxi")
    dma("s", T.xin[:, :], T.x[:, :], "d_x", "", "xin")
    dma("s", T.ut[:, :], T.u[:, :], "d_u", "", "ut")
    dma("s", T.wq[:, :].bitcast(dt.uint8), T.wc[:, :], "d_wc", "", "wq")
    dma("s", T.wsb[:, :], T.ws[:, :], "d_ws", "", "wsb")
    dma("s", T.vt[:, :], T.v[:, :], "d_v", "", "vt")

    op("g", lambda: g.iota(T.jp[:, :], [[0, 20], [1, 16]], 0, -1), "", "jp")
    op("g", lambda: g.iota(T.iotac[:, :], [[1, C]], -160, 0, allow_small_or_imprecise_dtypes=True), "", "iotac")
    send(partner[0], [(T.rnx[:, :], T.nxi[:, :])], "r_nx", "nxi")
    landed("r_nx", NE, "rnx")
    MS(T.ones[:, :], 1.0, "ones")
    op("g", lambda: g.affine_select(T.ef[:, :], T.ones[:, :], [[-1, 516]], A.is_equal, 0.0, 3, 4), "ones", "ef")
    op("g", lambda: g.iota(T.c16[:, :], [[16, 8]], 0, 0), "", "c16")
    MS(T.rst[:, :], 1.0, "rst")
    MS(T.rst[:, 0:C:16], 0.0, "rst")
    op("g", lambda: g.iota(T.jf[:, :], [[1, C]], 0, 0, allow_small_or_imprecise_dtypes=True), "", "jf")
    MS(T.of[:, 0:1], -160.0 * 2.0 ** -96, "of0")
    MS(T.ou[:, :], 0, "ou")
    MS(T.zero[:, :], 0.0, "zero")
    MS(T.low0[:, :], 0.0, "low0")
    MS(T.low1[:, :], 0.0, "low1")
    TS(T.jpa[:, :], T.jp[:, :], 15, None, A.bitwise_and, None, "jp", "jpa")
    TS(T.M[:, :], T.jpa[:, :], 0.0, None, A.is_equal, None, "jpa", "M")

    fillers = []

    def gap(n=1):
        for _ in range(n):
            if fillers: fillers.pop(0)()

    def conv(pieces, finish):
        b = turn[0] = 1 - turn[0]
        pm, s, kp, ks = T["pm%d" % b], T["sc%d" % b], "pm%d" % b, "sc%d" % b
        at, keys = 0, []
        for i, (win, off, rd, n) in enumerate(pieces):
            k = kp if i == 0 else "%s_%d" % (kp, i)
            TT(pm[:, at:at + n], win.indirect(off), T.M[:, 0:n], A.mult, rd + " M", kp if i == 0 else k)
            keys.append(k)
            at += n
        gap()
        SCAN(s[:, 0:at], T.rst[:, 0:at], pm[:, 0:at], 0.0, A.mult, A.add, " ".join(keys) + " rst", ks)
        gap()
        finish(s[:, 15:at:16], ks)
        gap()

    S96, P96 = 2.0 ** -96, 2.0 ** 96

    def to_list(out, wr):
        return lambda v, k: TS(out, v, P96, 160.0, A.mult, A.add, k, wr)

    def weigh(src, rd, finish):
        b = turn[0] = 1 - turn[0]
        w, k = T["wc%d" % b], "wc%d" % b
        SCAN(w[:, :], T.dR[:, :], src, 0.0, A.mult, A.add, rd + " dR", k)
        gap()
        finish(w[:, 15:C:16], k)
        gap()

    def to_wlist(out, wr):
        return lambda v, k: TS(out, v, T.wn[:, 15:16], 160.0, A.mult, A.add, k + " wn", wr)

    RK = {m: T.rk[:, C * i:C * i + C] for i, m in enumerate(POW)}
    LK = {m: T.lk[:, 20 * i:20 * i + 20] for i, m in enumerate([1, 4, 16])}
    OLALL = "ol0 ol1 ol2 ol3 ol4 ol5"

    def times(m, by):
        AC(RK[m + by], RK[m].indirect(LK[by]), "rk%d lk%d" % (m, by), "rk%d" % (m + by))

    def listed(m):
        weigh(RK[m], "rk%d" % m, to_wlist(LK[m], "lk%d" % m))

    def digit(l, d, m, lst, k):
        TT(T.og[:, 16 * d - 16:16 * d], RK[m].indirect(lst), T["low%d" % l][:, 16 * d - 16:16 * d], A.mult, "rk%d low%d " % (m, l) + k, "og%d" % d)

    def digits(l, out, wr):
        op("v", lambda: ve.tensor_reduce(T.ov[:, l:l + 1], T.og[:, :], AxisListType.X, A.add), "og1 og2 og3", "ov%d" % l)
        gap()
        TS(T.of[:, l + 1:l + 2], T.of[:, l:l + 1], T.nb[:, l:l + 1], T.ov[:, l:l + 1], A.mult, A.add, "of%d nb%d ov%d" % (l, l, l), "of%d" % (l + 1))
        gap()
        TS(out, T.of[:, l + 1:l + 2], P96, 160.0, A.mult, A.add, "of%d" % (l + 1), wr)

    def xname(r): return T["xq%d" % r], T["xs%d" % r], "xq%d" % r

    def quant_x(r):
        q, s, k = xname(r)
        t, tk = (T.xin, "xin") if r == 0 else (T.xt, "xt0 xt1 xt2 xt3")
        QZ(q[:, :], s[:, :], t[:, :], tk, k)

    def quant_e(b):
        QZ(T.eq[:, 128 * b:128 * b + 128], T.es[:, 128 * b:128 * b + 128], T.ef[:, 3 - b:515 - b], "ef", "eq%d" % b)

    def spread(r, q, s, k, banks):
        for b in range(4):
            MM(T["ps%d" % banks[b]][:, 0:C], T.eq[:, 128 * b:128 * b + 128], T.es[:, 128 * b:128 * b + 128], q[:, :], s[:, :], "eq%d " % b + k, "ps%d" % banks[b])

    NEAR, FAR = [1, 2, 3, 4], [5, 6, 7, 0]

    def start(r):
        q, s, k = xname(r)
        send(partner[r], [(T["rq%d" % r][:, :].bitcast(dt.uint8), q[:, :].bitcast(dt.uint8)), (T["rs%d" % r][:, :], s[:, :])], "r_x%d" % r, k)
        landed("r_x%d" % r, 2 * NE, "rq%d" % r)

    def scores(r):
        q, s, k = xname(r)
        for p in (0, 7):
            MM(T["ps%d" % p][:, 0:C], T.uw[:, :], T.uws[:, :], q[:, :], s[:, :], "uw " + k, "ps%d" % p)

    def unpack(b):
        AC(PLN(T.tb, b), T["ps%d" % NEAR[b]][:, 0:C], "ps%d" % NEAR[b], "tb%d" % b, 0.5)

    def unpack_far(r):
        q, s, k = T["rq%d" % r], T["rs%d" % r], "rq%d" % r
        spread(r, q, s, k, FAR)
        for b in range(4):
            AC(PLN(T.tp, b), T["ps%d" % FAR[b]][:, 0:C], "ps%d" % FAR[b], "tp%d" % b, 0.5)

    def guests(r):
        if r == 0: return T.gl[:, :], T.hl[:, :], "gl", "hl"
        return T["glab%d" % r][:, 0:20], T["glab%d" % r][:, 20:40], "glab%d" % r, "glab%d" % r

    def f_u(r):
        TS(T.uu[:, :], T.ps0[:, 0:C], 0.0, None, A.is_gt, None, "ps0", "uu")
        op("a", lambda: sc.activation(T.sg[:, :], T.ps7[:, 0:C], ACT.Sign), "ps7", "sg")

    def f_sv(r):
        gL, hL, gk, hk = guests(r)
        TT(T.svc[:, :], T.uu[:, :].indirect(hL), T.sg[:, :], A.is_ge, "uu sg " + hk, "svc")

    def f_lv():
        SCAN(T.lvs[:, :], T.d3[:, :], T.svc[:, :], 0.0, A.mult, A.add, "svc d3", "lvs")
        gap()
        TS(T.lv[:, :], T.lvs[:, 15:C:16], T.thr[:, 0:1], None, A.is_lt, None, "lvs thr", "lv")

    TC(LK[1], T.nxi[:, :], "nxi", "lk1")
    AC(RK[1], T.iotac[:, :].indirect(LK[1]), "iotac lk1", "rk1", S96)
    for d in range(1, 4):
        TC(T.low0[:, 16 * d - 16 + d:16 * d:4], T.M[:, d:16:4], "M", "low0")
        TC(T.low1[:, 16 * d - 16 + 4 * d:16 * d - 12 + 4 * d], T.M[:, 4 * d:4 * d + 4], "M", "low1")
    op("v", lambda: ve.tensor_reduce(T.nb[:, 0:1], T.M[:, 0:16:4], AxisListType.X, A.add), "M", "nb0")
    op("v", lambda: ve.tensor_reduce(T.nb[:, 1:2], T.M[:, 0:4], AxisListType.X, A.add), "M", "nb1")
    times(1, 1); times(2, 1); times(3, 1)
    AC(T.iotaT[:, :], T.iotac[:, :], "iotac", "iotaT", S96)
    TS(T.dR[:, :], T.M[:, :], -16384.0, 16384.0, A.mult, A.add, "M", "dR")
    TS(T.dI[:, :], T.M[:, 0:16], -2.0 ** -14, 2.0 ** -14, A.mult, A.add, "M", "dI")
    TS(T.mP[:, :], T.M[:, 0:16], P96, None, A.mult, None, "M", "mP")
    digit(0, 1, 1, T.ou[:, 0:1], "ou")
    SCAN(T.wn[:, :], T.dI[:, :], T.mP[:, :], 0.0, A.mult, A.add, "dI mP", "wn")
    MS(T.cb[:, 0:1], -160.0, "cb0")
    digit(0, 2, 2, T.ou[:, 0:1], "ou")
    TS(T.wn2[:, :], T.wn[:, 15:16], 2.0, None, A.mult, None, "wn", "wn2")
    TS(T.d3[:, :], T.M[:, :], -3.0, 3.0, A.mult, A.add, "M", "d3")
    quant_e(0); quant_e(1)
    digit(0, 3, 3, T.ou[:, 0:1], "ou")
    quant_e(2); quant_e(3)
    fillers += [lambda: TC(T.ul[:, :], T.c16[:, :], "c16", "ul"),
                lambda: MS(T.fi[:, 0:1], 0.0, "fi0")]
    listed(4)
    times(4, 4); times(8, 4); times(12, 4)
    fillers += [lambda: SCAN(T.th3[:, :], T.d3[:, 0:16], T.M[:, 0:16], 0.0, A.mult, A.add, "d3 M", "th3"),
                lambda: MS(T.fi[:, 1287:1288], 1.0, "fi1")]
    digits(0, T.ou1[:, 0:1], "ou1")
    TS(T.thr[:, :], T.th3[:, 15:16], 0.75, None, A.mult, None, "th3", "thr")
    digit(1, 1, 4, T.ou1[:, 0:1], "ou1")
    quant_x(0)
    start(0)
    digit(1, 2, 8, T.ou1[:, 0:1], "ou1")
    QZ(T.uq[:, :], T.us[:, :], T.ut[:, :], "ut", "uq")
    TC(T.uw[:, :].bitcast(dt.uint32), T.uq[:, :].bitcast(dt.uint32).indirect(T.ul[:, :]), "uq ul", "uwc")
    digit(1, 3, 12, T.ou1[:, 0:1], "ou1")
    op("a", lambda: sc.activation(T.uws[:, :], T.us[:, :].indirect(T.ul[:, :]), ACT.Copy), "uq ul uwc", "uw")
    listed(16)
    scores(0)
    times(16, 16); times(32, 16); times(48, 16)
    fillers += [lambda: TC(T.gl[:, :], T.rnx[:, :], "rnx", "gl")]
    digits(1, T.ol[:, 0:1], "ol0")
    spread(0, T.xq0, T.xs0, "xq0", NEAR)
    S20 = 2.0 ** -20
    AC(T.jS[:, :], T.jf[:, :], "jf", "jS", S20)
    ID(T.KE[:, :], T.jf[:, :], 641 * 512 * S20, 1024 * S20, "jf", "KE")
    op("v", lambda: ve.tensor_copy(T.hr[:, :].indirect(T.gl[:, :]), T.iotaT[:, :]), "gl iotaT", "hr")
    conv([(RK[16 * d], T.ol[:, 0:1], "rk%d ol0" % (16 * d), 16) for d in range(1, 4)], to_list(T.ol[:, 1:4], "ol1"))
    for i in range(4):
        if i == 0: fillers += [lambda: f_u(0)]
        if i == 1: weigh(T.hr[:, :], "hr", to_wlist(T.hl[:, :], "hl"))
        if i == 1:
            ID(T.KO[:, :], T.jf[:, :], 642 * 512 * S20, 1024 * S20, "jf", "KO")
            AC(T.M20[:, :], T.M[:, :], "M", "M20", 2.0 ** 20)
            AC(T.rst2[:, 0:C], T.rst[:, :], "rst", "rst2a")
        if i == 2: fillers += [lambda: f_sv(0)]
        if i == 3: fillers += [lambda: f_lv()]
        conv([(RK[64], T.ol[:, 4 * i:4 * i + 4], "rk64 " + ("ol0 ol1" if i == 0 else "ol%d" % (i + 1)), 64)], to_list(T.ol[:, 4 * i + 4:4 * i + 8], "ol%d" % (i + 2)))
    gap(len(fillers))

    def slots(r):
        gL, hL, gk, hk = guests(r)
        AC(T.gsv[:, :], T.svc[:, :].indirect(gL), "svc " + gk, "gsv")
        (TC if r else AC)(T.vf[:, 0:2 * C:2], T.svc[:, :].indirect(T.ol[:, :]), "svc " + OLALL, "vfa")
        ID(T.vf[:, 1:2 * C:2], T.gsv[:, :].indirect(T.ol[:, :]), 1.0, -1.0, "gsv " + OLALL, "vfb")

    def holes():
        ID(T.nvf[:, :], T.vf[:, :], 1.0, -1.0, "vfa vfb", "nvf")

    def cap_even(): TT(T.cap[:, 0:2 * C:2], T.jS[:, :].indirect(T.ol[:, :]), T.KE[:, :], A.add, "jS KE " + OLALL, "capa")

    def cap_odd(): TT(T.cap[:, 1:2 * C:2], T.gS[:, :].indirect(T.ol[:, :]), T.KO[:, :], A.add, "gS KO " + OLALL, "capb")

    def guest_cols(r):
        gL, hL, gk, hk = guests(r)
        AC(T.gS[:, :], T.jS[:, :].indirect(gL), "jS " + gk, "gS")

    def host_at(r):
        gL, hL, gk, hk = guests(r)
        AC(T.phr[:, :], T.posr[:, :].indirect(hL), "posr " + hk, "phr")

    def host_place():

        def fin(v, k):
            TS(T.ph2[:, :], v, T.wn2[:, 0:1], 321.0, A.mult, A.add, k + " wn2", "ph2")
            gap()
            TT(T.dq[:, :], T.ph2[:, :], T.pos2[:, :], A.subtract, "ph2 pos2", "dq")
        weigh(T.phr[:, :], "phr", fin)

    slots(0)
    op("v", lambda: ve.tensor_copy(T.posr[:, :].indirect(T.ol[:, :]), T.iotaT[:, :]), "iotaT " + OLALL, "posr")
    host_at(0)
    guest_cols(0)
    holes()
    AC(T.rst2[:, C:], T.rst[:, :], "rst", "rst2b")
    for b in range(4): unpack(b)
    fillers += [cap_even]
    weigh(T.posr[:, :], "posr", lambda v, k: TS(T.pos2[:, :], v, T.wn2[:, 0:1], 320.0, A.mult, A.add, k + " wn2", "pos2"))
    fillers += [cap_odd]
    host_place()

    for r in range(3):
        lab, rlab, lk, rk = T["lab%d" % r], T["rlab%d" % r], "lab%d" % r, "rlab%d" % r
        last = r == 2
        if r:
            quant_x(r)
            start(r)
            scores(r)
            q, s, k = xname(r)
            spread(r, q, s, k, NEAR)
            cap_even()
            f_u(r)
            unpack(0)
            f_sv(r)
            slots(r)
            holes()
            fillers += [cap_odd]
            f_lv()
            gap(len(fillers))
            unpack(1); unpack(2); unpack(3)
        unpack_far(r)
        TT(T.t1[:, :], T.lv[:, :], T.dq[:, :], A.mult, "lv dq", "t1")
        TT(T.t2[:, :], T.t1[:, :], T.pos2[:, :], A.add, "t1 pos2", "t2")
        SCAN(T.fi[:, 1:641], T.vf[:, :], T.cap[:, :], 0.0, A.max, A.min, "vfa vfb capa capb", "fif")
        TC(T.ql[:, :], T.t2[:, :], "t2", "ql")
        SCAN(T.fi[:, 1286:646:-1], T.nvf[:, ::-1], T.cap[:, ::-1], 1.0, A.min, A.max, "nvf capa capb", "fib")
        TT(T.xm[:, C:], T.fi[:, 0:640].indirect(T.ql[:, :]), T.M20[:, :], A.mult, "fif fi0 ql M20", "xmb")
        TT(T.xm[:, 0:C], T.fi[:, 648:1288].indirect(T.ql[:, :]), T.M20[:, :], A.mult, "fib fi1 ql M20", "xma")
        TS(T.wr[:, :], T.fi[:, 640:648:7], 2.0 ** 20, None, A.mult, None, "fif fib", "wr")
        SCAN(T.xsc[:, :], T.rst2[:, :], T.xm[:, :], 0.0, A.mult, A.add, "rst2a rst2b xma xmb", "xsc")
        TS(T.di[:, 0:20], T.xsc[:, 15:C:16], -327680.0, T.wr[:, 1:2], A.add, A.min, "xsc wr", "dia")
        TS(T.di[:, 20:40], T.xsc[:, C + 15:2 * C:16], 327680.0, T.wr[:, 0:1], A.add, A.max, "xsc wr", "dib")
        TS(T.da[:, :], T.di[:, :], 511, None, A.bitwise_and, None, "dia dib", "da")
        TC(lab[:, :], T.da[:, :], "da", lk)
        send(partner[r], [(rlab[:, :], lab[:, :])], "r_l%d" % r, lk)
        landed("r_l%d" % r, NE, rk)
        if not last:
            n = r + 1
            send(partner[n], [(T["glab%d" % n][:, :], lab[:, :])], "r_g%d" % n, lk)
            landed("r_g%d" % n, NE, "glab%d" % n)
        a, b_, ra, rb = lab[:, 0:20], lab[:, 20:40], rlab[:, 0:20], rlab[:, 20:40]
        def own_b(b): AC(PLN(T.gb, b), PLN(T.tb, b).indirect(b_), "tb%d " % b + lk, "gb%d" % b)

        if not last:
            SCAN(T.cb[:, 1:641], T.vf[:, :], T.zero[:, :], -160.0, A.add, A.add, "vfa vfb zero", "cb")
            TS(T.posr[:, :], T.cb[:, 0:640].indirect(T.ql[:, :]), S96, None, A.mult, None, "cb cb0 ql", "posr")

            def fin(v, k):
                TS(T.pu[:, :], v, T.wn[:, 15:16], 160.0, A.mult, A.add, k + " wn", "pu")
                TS(T.pos2[:, :], v, T.wn2[:, 0:1], 320.0, A.mult, A.add, k + " wn2", "pos2")
            weigh(T.posr[:, :], "posr", fin)
            op("v", lambda: ve.tensor_copy(T.ordr[:, :].indirect(T.pu[:, :]), T.iotaT[:, :]), "pu iotaT", "ordr")
        for b in range(4): own_b(b)
        if last:
            QZ(T.vq[:, :], T.vs[:, :], T.vt[:, :], "vt", "vq")
        AC(T.zb[:, 0:160], PLN(T.tp, 0).indirect(rlab[:, 20:30]), "tp0 " + rk, "zb0a")
        TC(T.zb[:, 160:C], PLN(T.tp, 0).indirect(rlab[:, 30:40]), "tp0 " + rk, "zb0")
        for b in range(1, 4):
            AC(PLN(T.zb, b), PLN(T.tp, b).indirect(rb), "tp%d " % b + rk, "zb%d" % b)
        for b in range(4):
            TT(T.zt[:, b:4 * C:4], PLN(T.tp, b).indirect(ra), PLN(T.zb, b), A.add, "tp%d zb%d " % (b, b) + rk + (" zb0a" if b == 0 else ""), "zt%d" % b)
        QZ(T.zq[:, :], T.zs[:, :], T.zt[:, :], "zt0 zt1 zt2 zt3", "zq")
        for b in range(4):
            MM(T["ps%d" % (b + 1)][:, 0:C], T.wq[:, 128 * b:128 * b + 128], T.wsb[:, 128 * b:128 * b + 128], T.zq[:, :], T.zs[:, :], "wq wsb zq", "ps%d" % (b + 1))
        if not last:
            host_at(r + 1)
            weigh(T.ordr[:, :], "ordr", to_wlist(T.ol[:, :], OLALL))
            host_place()
        for b in range(4):
            AC(PLN(T.hb, b), T["ps%d" % (b + 1)][:, 0:C], "ps%d" % (b + 1), "hb%d" % b, 2.0 ** -6)
        for b in range(4):
            TT(T.xt[:, b:4 * C:4], PLN(T.hb, b).indirect(a), PLN(T.gb, b), A.add, "hb%d gb%d " % (b, b) + lk, "xt%d" % b)
        if not last:
            guest_cols(r + 1)
        else:
            AC(T.nrr[:, :], T.jf[:, :].indirect(a), "jf " + lk, "nrr")
            dma("s", T.nr[:, :], T.nrr[0:128:16, :], "d_out", "nrr", "nr")

    q, s, k = xname(3)
    quant_x(3)
    MM(T.ps0[:, 0:C], T.vq[:, :], T.vs[:, :], q[:, :], s[:, :], "vq " + k, "ps0")
    dma("s", T.oc[:, :], q[:, :].bitcast(dt.uint8), "d_out", k, "oc")
    for i in range(4):
        dma("a" if i % 2 else "s", T.osc[4 * i:4 * i + 4, :], s[32 * i:32 * i + 4, :], "d_out", k, "osc%d" % i)
    TC(T.yo[:, :], T.ps0[:, 0:C], "ps0", "yo")
    dma("s", T.y[:, :], T.yo[:, :], "d_out", "yo", "y")
    for name in SEMAPHORES:
        if count.get(name): need("s", (name, count[name], {}))
